import numpy as np
import ml_dtypes


def mxq(x, axis, fmt="e4m3"):
    dtype, down = {"e4m3": (ml_dtypes.float8_e4m3fn, 7), "e5m2": (ml_dtypes.float8_e5m2, 14)}[fmt]
    v = np.moveaxis(np.asarray(x, np.float32).astype(ml_dtypes.bfloat16).astype(np.float64), axis, -1)
    blocks = v.reshape(v.shape[:-1] + (-1, 32))
    amax = np.abs(blocks).max(-1, keepdims=True)
    byte = np.maximum(np.where(amax > 0, np.frexp(amax)[1] - 1 + 127, 0) - down, 1)
    scale = np.exp2(byte - 127.0)
    codes = (blocks / scale).astype(np.float32).astype(dtype).astype(np.float64)
    return np.moveaxis((codes * scale).reshape(v.shape), -1, axis)


WIDE = False


def mx_kscale(k):
    if not WIDE:
        return np.ones(k)
    levels = np.array([10, -10, 5, -5, 0])
    if k % 512:
        return np.exp2(np.random.permutation(np.resize(levels, k // 32))).repeat(32)
    a = np.empty((k // 512, 16))
    for p in range(k // 512):
        a[p, :8] = np.random.permutation(np.resize(levels, 8))
        for g in range(8):
            far = levels[np.abs(levels - a[p, g]) >= 10]
            a[p, g + 8] = far[np.random.randint(len(far))]
    return np.exp2(a.ravel()).repeat(32)


def f64(x):
    return np.asarray(x).astype(np.float64)


def striped8(idx):
    return np.asarray(idx).reshape(8, -1, 16).transpose(0, 2, 1).reshape(128, -1).astype(np.uint16)


def unstriped8(offs):
    return offs.reshape(8, 16, -1).transpose(0, 2, 1).reshape(8, -1).astype(np.int64)


def pick8(x, idx, run):
    r = np.arange(len(x))
    return x[r[:, None], idx[r % (8 * run) // run]]


E2M1 = np.array([0.0, 0.5, 1.0, 1.5, 2.0, 3.0, 4.0, 6.0, -0.0, -0.5, -1.0, -1.5, -2.0, -3.0, -4.0, -6.0])


def pack_weight(w, fmt):
    k, n = w.shape
    w = f64(np.asarray(w, np.float32).astype(ml_dtypes.bfloat16)).reshape(k // 32, 32, n)
    amax = np.abs(w).max(1)
    if fmt == "e4m3":
        byte = np.frexp(amax)[1] - 1 + 127 - 7
    else:
        mant, ex = np.frexp(amax / 6.0)
        byte = np.where(mant > 0.5, ex, ex - 1) + 127
    byte = np.clip(np.where(amax > 0, byte, 1), 1, 254)
    scaled = (w * np.exp2(127.0 - byte)[:, None, :]).reshape(k, n).astype(np.float32)
    by_word = np.ascontiguousarray(scaled.reshape(k // 512, 128, 4, n).transpose(0, 1, 3, 2))
    if fmt == "e4m3":
        words = by_word.astype(ml_dtypes.float8_e4m3fn).view(np.uint8)
    else:
        c = by_word.astype(ml_dtypes.float4_e2m1fn).view(np.uint8) & 0xF
        words = (c[..., 0::2] | (c[..., 1::2] << 4)).reshape(k // 512, 128, 2 * n)
    return np.ascontiguousarray(words), np.ascontiguousarray(byte.astype(np.uint8).reshape(k // 512, 16, n))


def unpack_weight(words, scales, fmt):
    g, _, n = scales.shape
    words = np.ascontiguousarray(words).reshape(g, 128, n, -1)
    if fmt == "e4m3":
        vals = words.view(ml_dtypes.float8_e4m3fn).astype(np.float64)
    else:
        nib = np.empty((g, 128, n, 4), np.uint8)
        nib[..., 0::2] = words & 0xF
        nib[..., 1::2] = words >> 4
        vals = E2M1[nib]
    vals = vals * np.repeat(np.exp2(scales.astype(np.float64) - 127.0), 8, axis=1)[..., None]
    return vals.transpose(0, 1, 3, 2).reshape(g * 512, n)


D, T, I, Q = 512, 1024, 512, 128


def setup_inputs():
    n = np.random.standard_normal
    idx = np.stack([np.random.permutation(T)[:I] for _ in range(8)])
    idx2 = np.stack([np.random.permutation(T)[:I] for _ in range(8)])
    idx3 = np.stack([np.random.permutation(T)[:I] for _ in range(8)])
    idx4 = np.stack([np.random.permutation(T)[:I] for _ in range(8)])
    fd = mx_kscale(D)
    keysp = pack_weight(n((D, T)) / fd[:, None], "e4m3")
    return {
        "query": (n((D, Q)) * 0.9 / np.sqrt(D) * fd[:, None]).astype(np.float32),
        "keys_words": keysp[0],
        "keys_scales": keysp[1],
        "lam": (np.random.uniform(0.7, 1.3, (Q, 1))).astype(np.float32),
        "old": (1.0 * n((Q, T))).astype(np.float32),
        "offs": striped8(idx),
        "offs2": striped8(idx2),
        "offs3": striped8(idx3),
        "offs4": striped8(idx4),
    }


def reference(query, keys_words, keys_scales, lam, old, offs, offs2, offs3, offs4):
    idx = unstriped8(offs)
    idx2 = unstriped8(offs2)
    idx3 = unstriped8(offs3)
    idx4 = unstriped8(offs4)
    keysu = unpack_weight(keys_words, keys_scales, "e4m3")
    queryq = mxq(f64(query), 0, "e4m3")
    a = queryq.T @ keysu
    w = pick8(a, idx, 16) * f64(lam) - np.abs(pick8(a, idx2, 16) - pick8(a, idx3, 16))
    f1 = np.zeros((Q, T))
    f1[np.arange(Q)[:, None], idx[np.arange(Q) % 128 // 16]] = w
    f2 = f1 + f64(old)
    y = pick8(f2, idx4, 16)
    return y

@@ -1,0 +1,126 @@
+from contextlib import ExitStack
+
+import concourse.mybir as mybir
+
+D, T, I, Q = 512, 1024, 512, 128
+FLOPS = 2 * D * Q * T
+
+F32 = mybir.dt.float32
+BF16 = mybir.dt.bfloat16
+I32 = mybir.dt.int32
+U32 = mybir.dt.uint32
+U16 = mybir.dt.uint16
+U8 = mybir.dt.uint8
+FP8X4 = mybir.dt.float8_e4m3fn_x4
+ALU = mybir.AluOpType
+ACT = mybir.ActivationFunctionType
+
+P = 128
+PACK = 4
+GROUP = 16
+HALF = I // 2
+KEY_LOADS = 2
+WIDTHS = (256, 256, 256, 128, 128)
+
+
+def tile_attend_betweentwo_lean_through_heads_kernel(tc, query, keys_words, keys_scales, lam, old, offs, offs2, offs3, offs4, out):
+    nc = tc.nc
+    with ExitStack() as ctx:
+        sb = ctx.enter_context(tc.tile_pool(name="sb", bufs=1))
+        ps = ctx.enter_context(tc.psum_pool(name="ps", bufs=1))
+
+        k_scales = sb.tile([P, T], U8, align_bytes=64)
+        nc.vector.memset(k_scales[:].bitcast(I32), 0)
+
+        q_raw = sb.tile([P, PACK, Q], F32)
+        nc.sync.dma_start(out=q_raw[:], in_=query.rearrange("(p j) q -> p j q", j=PACK))
+        for quad in range(4):
+            nc.sync.dma_start(
+                out=k_scales[32 * quad : 32 * quad + 4, :].bitcast(I32),
+                in_=keys_scales[0, 4 * quad : 4 * quad + 4, :].bitcast(I32),
+            )
+        words_hbm = keys_words[0].rearrange("p n t -> p (n t)")
+        per_load = T // KEY_LOADS
+        k_words = []
+        for c in range(KEY_LOADS):
+            words = sb.tile([P, per_load], I32, align_bytes=64, name=f"k_words{c}")
+            nc.sync.dma_start(out=words[:], in_=words_hbm[:, PACK * per_load * c : PACK * per_load * (c + 1)].bitcast(I32))
+            k_words.append(words)
+
+        list3 = sb.tile([P, I // GROUP], U16)
+        nc.sync.dma_start(list3[:], offs3)
+        list1 = sb.tile([P, I // GROUP], U16)
+        nc.sync.dma_start(list1[:], offs)
+        list2 = sb.tile([P, I // GROUP], U16)
+        nc.sync.dma_start(list2[:], offs2)
+        lam_col = sb.tile([P, 1], F32)
+        nc.gpsimd.dma_start(out=lam_col[:], in_=lam)
+        old_sb = sb.tile([P, T], F32)
+        nc.sync.dma_start(out=old_sb[:], in_=old)
+        list4 = sb.tile([P, I // GROUP], U16)
+        nc.sync.dma_start(list4[:], offs4)
+
+        f1 = sb.tile([P, T], F32)
+        nc.vector.memset(f1[:], 0.0)
+        lam_wide = sb.tile([P, HALF], F32)
+        nc.scalar.activation(lam_wide[:], lam_col[:].to_broadcast([P, HALF]), ACT.Copy, scale=-1.0)
+
+        q_bf = sb.tile([P, Q, PACK], BF16, align_bytes=64)
+        nc.vector.tensor_copy(out=q_bf[:, :80, :], in_=q_raw[:, :, :80].rearrange("p j q -> p q j"))
+        nc.scalar.copy(q_bf[:, 80:, :], q_raw[:, :, 80:].rearrange("p j q -> p q j"))
+        q_words = sb.tile([P, Q], U32, align_bytes=64)
+        q_scales = sb.tile([P, Q], U8, align_bytes=64)
+        nc.vector.quantize_mx(out=q_words[:].bitcast(FP8X4), scales=q_scales[:], in_=q_bf[:].rearrange("p q j -> p (q j)"))
+
+        a = sb.tile([P, T], F32)
+        start = 0
+        for b, width in enumerate(WIDTHS):
+            bank = ps.tile([P, width], F32, name=f"bank{b}")
+            c, first = divmod(start, per_load)
+            cols = slice(start, start + width)
+            start += width
+            nc.tensor.matmul_mx(
+                out=bank[:],
+                lhsT=q_words[:].bitcast(FP8X4),
+                lhsT_scale=q_scales[:],
+                rhs=k_words[c][:, first : first + width].bitcast(FP8X4),
+                rhs_scale=k_scales[:, cols],
+                start=True,
+                stop=True,
+            )
+            if b % 2 == 1:
+                nc.scalar.copy(a[:, cols], bank[:])
+            else:
+                nc.vector.tensor_copy(a[:, cols], bank[:])
+
+        def picked(window, offsets, h):
+            return window[:].indirect(offsets[:, h * HALF // GROUP : (h + 1) * HALF // GROUP])
+
+        def half_tile(name, h):
+            return sb.tile([P, HALF], F32, name=f"{name}{h}")
+
+        third = [half_tile("third", h) for h in range(2)]
+        diff = [half_tile("diff", h) for h in range(2)]
+        dist = [half_tile("dist", h) for h in range(2)]
+        scaled = [half_tile("scaled", 0), diff[0]]
+        first1 = half_tile("first", 1)
+
+        nc.scalar.activation(third[0][:], picked(a, list3, 0), ACT.Copy)
+        nc.vector.tensor_tensor(scaled[0][:], picked(a, list1, 0), lam_wide[:], ALU.mult)
+        nc.scalar.activation(third[1][:], picked(a, list3, 1), ACT.Copy)
+        for h in range(2):
+            nc.vector.tensor_tensor(diff[h][:], picked(a, list2, h), third[h][:], ALU.subtract)
+        nc.scalar.activation(first1[:], picked(a, list1, 1), ACT.Copy)
+        nc.scalar.activation(dist[0][:], diff[0][:], ACT.Abs)
+        nc.vector.tensor_tensor(picked(f1, list1, 0), scaled[0][:], dist[0][:], ALU.add)
+        nc.scalar.activation(scaled[1][:], first1[:], ACT.Copy, scale=lam_wide[:, 0:1])
+        nc.scalar.activation(dist[1][:], diff[1][:], ACT.Abs)
+        nc.vector.tensor_tensor(picked(f1, list1, 1), scaled[1][:], dist[1][:], ALU.add)
+
+        f2 = sb.tile([P, T], F32)
+        nc.vector.tensor_tensor(f2[:], old_sb[:], f1[:], ALU.subtract)
+        result = [half_tile("result", h) for h in range(2)]
+        nc.scalar.activation(result[0][:], picked(f2, list4, 0), ACT.Copy)
+        nc.scalar.dma_start(out=out[:, :HALF], in_=result[0][:])
+        nc.vector.tensor_copy(result[1][:], picked(f2, list4, 1))
+        nc.sync.dma_start(out=out[:, HALF:], in_=result[1][:])

@@ -29,15 +29,17 @@ def tile_attend_betweentwo_lean_through_heads_kernel(tc, query, keys_words, keys
         sb = ctx.enter_context(tc.tile_pool(name="sb", bufs=1))
         ps = ctx.enter_context(tc.psum_pool(name="ps", bufs=1))
 
-        k_scales = sb.tile([P, T], U8, align_bytes=64)
+        k_scales = sb.tile([P, T // 4], U8, align_bytes=64)
         nc.vector.memset(k_scales[:].bitcast(I32), 0)
 
         q_raw = sb.tile([P, PACK, Q], F32)
         nc.sync.dma_start(out=q_raw[:], in_=query.rearrange("(p j) q -> p j q", j=PACK))
+        list3 = sb.tile([P, I // GROUP], U16)
+        nc.sync.dma_start(list3[:], offs3)
         for quad in range(4):
             nc.sync.dma_start(
-                out=k_scales[32 * quad : 32 * quad + 4, :].bitcast(I32),
-                in_=keys_scales[0, 4 * quad : 4 * quad + 4, :].bitcast(I32),
+                out=k_scales[32 * quad : 32 * quad + 16, :].bitcast(I32),
+                in_=keys_scales[0, 4 * quad : 4 * quad + 4, :].bitcast(I32).rearrange("r (a c) -> a r c", a=4),
             )
         words_hbm = keys_words[0].rearrange("p n t -> p (n t)")
         per_load = T // KEY_LOADS
@@ -47,8 +49,6 @@ def tile_attend_betweentwo_lean_through_heads_kernel(tc, query, keys_words, keys
             nc.sync.dma_start(out=words[:], in_=words_hbm[:, PACK * per_load * c : PACK * per_load * (c + 1)].bitcast(I32))
             k_words.append(words)
 
-        list3 = sb.tile([P, I // GROUP], U16)
-        nc.sync.dma_start(list3[:], offs3)
         list1 = sb.tile([P, I // GROUP], U16)
         nc.sync.dma_start(list1[:], offs)
         list2 = sb.tile([P, I // GROUP], U16)
@@ -61,7 +61,7 @@ def tile_attend_betweentwo_lean_through_heads_kernel(tc, query, keys_words, keys
         nc.sync.dma_start(list4[:], offs4)
 
         f1 = sb.tile([P, T], F32)
-        nc.vector.memset(f1[:], 0.0)
+        nc.vector.memset(f1[:].bitcast(I32), 0)
         lam_wide = sb.tile([P, HALF], F32)
         nc.scalar.activation(lam_wide[:], lam_col[:].to_broadcast([P, HALF]), ACT.Copy, scale=-1.0)
 
@@ -84,7 +84,7 @@ def tile_attend_betweentwo_lean_through_heads_kernel(tc, query, keys_words, keys
                 lhsT=q_words[:].bitcast(FP8X4),
                 lhsT_scale=q_scales[:],
                 rhs=k_words[c][:, first : first + width].bitcast(FP8X4),
-                rhs_scale=k_scales[:, cols],
+                rhs_scale=k_scales[4 * (cols.start // 256) :, cols.start % 256 : cols.start % 256 + width],
                 start=True,
                 stop=True,
             )

from contextlib import ExitStack

import concourse.mybir as mybir

D, T, I, Q = 512, 1024, 512, 128
FLOPS = 2 * D * Q * T

F32 = mybir.dt.float32
BF16 = mybir.dt.bfloat16
I32 = mybir.dt.int32
U32 = mybir.dt.uint32
U16 = mybir.dt.uint16
U8 = mybir.dt.uint8
FP8X4 = mybir.dt.float8_e4m3fn_x4
ALU = mybir.AluOpType
ACT = mybir.ActivationFunctionType

P = 128
PACK = 4
GROUP = 16
HALF = I // 2
KEY_LOADS = 2
WIDTHS = (256, 256, 256, 128, 128)


def tile_attend_betweentwo_lean_through_heads_kernel(tc, query, keys_words, keys_scales, lam, old, offs, offs2, offs3, offs4, out):
    nc = tc.nc
    with ExitStack() as ctx:
        sb = ctx.enter_context(tc.tile_pool(name="sb", bufs=1))
        ps = ctx.enter_context(tc.psum_pool(name="ps", bufs=1))

        k_scales = sb.tile([P, T // 4], U8, align_bytes=64)
        nc.vector.memset(k_scales[:].bitcast(I32), 0)

        q_raw = sb.tile([P, PACK, Q], F32)
        nc.sync.dma_start(out=q_raw[:], in_=query.rearrange("(p j) q -> p j q", j=PACK))
        list3 = sb.tile([P, I // GROUP], U16)
        nc.sync.dma_start(list3[:], offs3)
        for quad in range(4):
            nc.sync.dma_start(
                out=k_scales[32 * quad : 32 * quad + 16, :].bitcast(I32),
                in_=keys_scales[0, 4 * quad : 4 * quad + 4, :].bitcast(I32).rearrange("r (a c) -> a r c", a=4),
            )
        words_hbm = keys_words[0].rearrange("p n t -> p (n t)")
        per_load = T // KEY_LOADS
        k_words = []
        for c in range(KEY_LOADS):
            words = sb.tile([P, per_load], I32, align_bytes=64, name=f"k_words{c}")
            nc.sync.dma_start(out=words[:], in_=words_hbm[:, PACK * per_load * c : PACK * per_load * (c + 1)].bitcast(I32))
            k_words.append(words)

        list1 = sb.tile([P, I // GROUP], U16)
        nc.sync.dma_start(list1[:], offs)
        list2 = sb.tile([P, I // GROUP], U16)
        nc.sync.dma_start(list2[:], offs2)
        lam_col = sb.tile([P, 1], F32)
        nc.gpsimd.dma_start(out=lam_col[:], in_=lam)
        old_sb = sb.tile([P, T], F32)
        nc.sync.dma_start(out=old_sb[:], in_=old)
        list4 = sb.tile([P, I // GROUP], U16)
        nc.sync.dma_start(list4[:], offs4)

        f1 = sb.tile([P, T], F32)
        nc.vector.memset(f1[:].bitcast(I32), 0)
        lam_wide = sb.tile([P, HALF], F32)
        nc.scalar.activation(lam_wide[:], lam_col[:].to_broadcast([P, HALF]), ACT.Copy, scale=-1.0)

        q_bf = sb.tile([P, Q, PACK], BF16, align_bytes=64)
        nc.vector.tensor_copy(out=q_bf[:, :80, :], in_=q_raw[:, :, :80].rearrange("p j q -> p q j"))
        nc.scalar.copy(q_bf[:, 80:, :], q_raw[:, :, 80:].rearrange("p j q -> p q j"))
        q_words = sb.tile([P, Q], U32, align_bytes=64)
        q_scales = sb.tile([P, Q], U8, align_bytes=64)
        nc.vector.quantize_mx(out=q_words[:].bitcast(FP8X4), scales=q_scales[:], in_=q_bf[:].rearrange("p q j -> p (q j)"))

        a = sb.tile([P, T], F32)
        start = 0
        for b, width in enumerate(WIDTHS):
            bank = ps.tile([P, width], F32, name=f"bank{b}")
            c, first = divmod(start, per_load)
            cols = slice(start, start + width)
            start += width
            nc.tensor.matmul_mx(
                out=bank[:],
                lhsT=q_words[:].bitcast(FP8X4),
                lhsT_scale=q_scales[:],
                rhs=k_words[c][:, first : first + width].bitcast(FP8X4),
                rhs_scale=k_scales[4 * (cols.start // 256) :, cols.start % 256 : cols.start % 256 + width],
                start=True,
                stop=True,
            )
            if b % 2 == 1:
                nc.scalar.copy(a[:, cols], bank[:])
            else:
                nc.vector.tensor_copy(a[:, cols], bank[:])

        def picked(window, offsets, h):
            return window[:].indirect(offsets[:, h * HALF // GROUP : (h + 1) * HALF // GROUP])

        def half_tile(name, h):
            return sb.tile([P, HALF], F32, name=f"{name}{h}")

        third = [half_tile("third", h) for h in range(2)]
        diff = [half_tile("diff", h) for h in range(2)]
        dist = [half_tile("dist", h) for h in range(2)]
        scaled = [half_tile("scaled", 0), diff[0]]
        first1 = half_tile("first", 1)

        nc.scalar.activation(third[0][:], picked(a, list3, 0), ACT.Copy)
        nc.vector.tensor_tensor(scaled[0][:], picked(a, list1, 0), lam_wide[:], ALU.mult)
        nc.scalar.activation(third[1][:], picked(a, list3, 1), ACT.Copy)
        for h in range(2):
            nc.vector.tensor_tensor(diff[h][:], picked(a, list2, h), third[h][:], ALU.subtract)
        nc.scalar.activation(first1[:], picked(a, list1, 1), ACT.Copy)
        nc.scalar.activation(dist[0][:], diff[0][:], ACT.Abs)
        nc.vector.tensor_tensor(picked(f1, list1, 0), scaled[0][:], dist[0][:], ALU.add)
        nc.scalar.activation(scaled[1][:], first1[:], ACT.Copy, scale=lam_wide[:, 0:1])
        nc.scalar.activation(dist[1][:], diff[1][:], ACT.Abs)
        nc.vector.tensor_tensor(picked(f1, list1, 1), scaled[1][:], dist[1][:], ALU.add)

        f2 = sb.tile([P, T], F32)
        nc.vector.tensor_tensor(f2[:], old_sb[:], f1[:], ALU.subtract)
        result = [half_tile("result", h) for h in range(2)]
        nc.scalar.activation(result[0][:], picked(f2, list4, 0), ACT.Copy)
        nc.scalar.dma_start(out=out[:, :HALF], in_=result[0][:])
        nc.vector.tensor_copy(result[1][:], picked(f2, list4, 1))
        nc.sync.dma_start(out=out[:, HALF:], in_=result[1][:])
